import numpy as np
import ml_dtypes

BF16 = ml_dtypes.bfloat16


def bf(x):
    return np.asarray(x, np.float32).astype(BF16)


def f32(x):
    return np.asarray(x, np.float32)


def f64(x):
    return np.asarray(x).astype(np.float64)


def striped(idx):
    return np.tile(idx.reshape(-1, 16).T, (8, 1))


S, K, M, N = 512, 256, 256, 64


def setup_inputs():
    return {"base": bf(np.random.standard_normal((M, S))), "x": bf(np.random.standard_normal((K, N))), "w": bf(np.random.standard_normal((K, M)) / np.sqrt(K)), "b": f32(0.5 * np.random.standard_normal((M, 1))), "offs": striped(np.random.permutation(S)[:N])}


def reference(base, x, w, b, offs):
    idx = offs[:16].T.reshape(-1)
    z = f64(base).copy()
    z[:, idx] += f64(w).T @ f64(x)
    return z + f64(b)

@@ -1,0 +1,62 @@
+import concourse.mybir as mybir
+from concourse.masks import make_identity
+
+BF16, F32, U16 = mybir.dt.bfloat16, mybir.dt.float32, mybir.dt.uint16
+ADD = mybir.AluOpType.add
+IDENTITY = mybir.ActivationFunctionType.Identity
+
+P = 128
+S = 512
+K = 256
+M = 256
+N = 64
+K_BLOCKS = K // P
+M_BLOCKS = M // P
+
+FLOPS = 2 * K * M * N
+
+
+def tile_scatter_matmul_kernel(tc, base, x, w, b, offs, out):
+    nc = tc.nc
+    with (
+        tc.tile_pool(name="held", bufs=1) as held,
+        tc.psum_pool(name="psum", bufs=1) as psum,
+    ):
+        offsets = held.tile([P, N // 16], U16, name="offsets")
+        nc.sync.dma_start(offsets[:], offs)
+
+        ident = held.tile([P, P], BF16, name="ident")
+        make_identity(nc, ident[:])
+
+        base_tiles = [held.tile([P, S], BF16, name=f"base{mb}") for mb in range(M_BLOCKS)]
+        nc.sync.dma_start(base_tiles[0][:], base[0:P, :])
+        nc.scalar.dma_start(base_tiles[1][:], base[P : 2 * P, :])
+
+        w_tile = held.tile([P, K_BLOCKS, M], BF16, name="w_tile")
+        nc.sync.dma_start(w_tile[:], w.rearrange("(kb p) m -> p kb m", p=P))
+        x_tile = held.tile([P, K_BLOCKS, N], BF16, name="x_tile")
+        nc.scalar.dma_start(x_tile[:], x.rearrange("(kb p) n -> p kb n", p=P))
+
+        bias = held.tile([P, M_BLOCKS], F32, name="bias")
+        with nc.allow_non_contiguous_dma(reason="one float32 to a partition and block"):
+            nc.scalar.dma_start(bias[:], b.rearrange("(mb p) o -> p (mb o)", p=P))
+
+        windows = [psum.tile([P, S], F32, name=f"window{mb}") for mb in range(M_BLOCKS)]
+        for mb in range(M_BLOCKS):
+            nc.tensor.matmul(windows[mb][:], ident[:], base_tiles[mb][:], start=True, stop=False)
+
+        for mb in range(M_BLOCKS):
+            for kb in range(K_BLOCKS):
+                nc.tensor.matmul(
+                    windows[mb][:].indirect(offsets[:]),
+                    w_tile[:, kb, mb * P : (mb + 1) * P],
+                    x_tile[:, kb, :],
+                    start=False,
+                    stop=(kb == K_BLOCKS - 1),
+                )
+
+        staged = [held.tile([P, S], F32, name=f"staged{mb}") for mb in range(M_BLOCKS)]
+        nc.vector.tensor_scalar(staged[0][:], windows[0][:], bias[:, 0:1], None, ADD)
+        nc.sync.dma_start(out[0:P, :], staged[0][:])
+        nc.scalar.activation(staged[1][:], windows[1][:], IDENTITY, bias=bias[:, 1:2])
+        nc.scalar.dma_start(out[P : 2 * P, :], staged[1][:])

@@ -13,6 +13,8 @@ N = 64
 K_BLOCKS = K // P
 M_BLOCKS = M // P
 
+WARMING_MATMULS = 5
+
 FLOPS = 2 * K * M * N
 
 
@@ -24,6 +26,12 @@ def tile_scatter_matmul_kernel(tc, base, x, w, b, offs, out):
     ):
         offsets = held.tile([P, N // 16], U16, name="offsets")
         nc.sync.dma_start(offsets[:], offs)
+
+        zeros = held.tile([P, S], BF16, name="zeros")
+        nc.vector.memset(zeros[:], 0.0)
+        unread = psum.tile([P, S], F32, name="unread")
+        for i in range(WARMING_MATMULS):
+            nc.tensor.matmul(unread[:], zeros[:, 0:P], zeros[:], start=True, stop=True)
 
         ident = held.tile([P, P], BF16, name="ident")
         make_identity(nc, ident[:])

@@ -12,8 +12,7 @@ M = 256
 N = 64
 K_BLOCKS = K // P
 M_BLOCKS = M // P
-
-WARMING_MATMULS = 5
+HALF = S // 2
 
 FLOPS = 2 * K * M * N
 
@@ -24,21 +23,15 @@ def tile_scatter_matmul_kernel(tc, base, x, w, b, offs, out):
         tc.tile_pool(name="held", bufs=1) as held,
         tc.psum_pool(name="psum", bufs=1) as psum,
     ):
-        offsets = held.tile([P, N // 16], U16, name="offsets")
-        nc.sync.dma_start(offsets[:], offs)
-
-        zeros = held.tile([P, S], BF16, name="zeros")
-        nc.vector.memset(zeros[:], 0.0)
-        unread = psum.tile([P, S], F32, name="unread")
-        for i in range(WARMING_MATMULS):
-            nc.tensor.matmul(unread[:], zeros[:, 0:P], zeros[:], start=True, stop=True)
-
         ident = held.tile([P, P], BF16, name="ident")
         make_identity(nc, ident[:])
 
         base_tiles = [held.tile([P, S], BF16, name=f"base{mb}") for mb in range(M_BLOCKS)]
         nc.sync.dma_start(base_tiles[0][:], base[0:P, :])
         nc.scalar.dma_start(base_tiles[1][:], base[P : 2 * P, :])
+
+        offsets = held.tile([P, N // 16], U16, name="offsets")
+        nc.sync.dma_start(offsets[:], offs)
 
         w_tile = held.tile([P, K_BLOCKS, M], BF16, name="w_tile")
         nc.sync.dma_start(w_tile[:], w.rearrange("(kb p) m -> p kb m", p=P))
@@ -48,6 +41,10 @@ def tile_scatter_matmul_kernel(tc, base, x, w, b, offs, out):
         bias = held.tile([P, M_BLOCKS], F32, name="bias")
         with nc.allow_non_contiguous_dma(reason="one float32 to a partition and block"):
             nc.scalar.dma_start(bias[:], b.rearrange("(mb p) o -> p (mb o)", p=P))
+
+        spare = held.tile([P, 2], F32, name="spare")
+        nc.vector.memset(spare[:, 0:1], 0.0)
+        nc.scalar.activation(spare[:, 1:2], spare[:, 0:1], IDENTITY)
 
         windows = [psum.tile([P, S], F32, name=f"window{mb}") for mb in range(M_BLOCKS)]
         for mb in range(M_BLOCKS):
@@ -64,7 +61,9 @@ def tile_scatter_matmul_kernel(tc, base, x, w, b, offs, out):
                 )
 
         staged = [held.tile([P, S], F32, name=f"staged{mb}") for mb in range(M_BLOCKS)]
-        nc.vector.tensor_scalar(staged[0][:], windows[0][:], bias[:, 0:1], None, ADD)
-        nc.sync.dma_start(out[0:P, :], staged[0][:])
-        nc.scalar.activation(staged[1][:], windows[1][:], IDENTITY, bias=bias[:, 1:2])
-        nc.scalar.dma_start(out[P : 2 * P, :], staged[1][:])
+        for half in range(2):
+            cols = slice(half * HALF, (half + 1) * HALF)
+            nc.vector.tensor_scalar(staged[0][:, cols], windows[0][:, cols], bias[:, 0:1], None, ADD)
+            nc.sync.dma_start(out[0:P, cols], staged[0][:, cols])
+            nc.scalar.activation(staged[1][:, cols], windows[1][:, cols], IDENTITY, bias=bias[:, 1:2])
+            nc.scalar.dma_start(out[P : 2 * P, cols], staged[1][:, cols])

@@ -12,7 +12,6 @@ M = 256
 N = 64
 K_BLOCKS = K // P
 M_BLOCKS = M // P
-HALF = S // 2
 
 FLOPS = 2 * K * M * N
 
@@ -61,9 +60,7 @@ def tile_scatter_matmul_kernel(tc, base, x, w, b, offs, out):
                 )
 
         staged = [held.tile([P, S], F32, name=f"staged{mb}") for mb in range(M_BLOCKS)]
-        for half in range(2):
-            cols = slice(half * HALF, (half + 1) * HALF)
-            nc.vector.tensor_scalar(staged[0][:, cols], windows[0][:, cols], bias[:, 0:1], None, ADD)
-            nc.sync.dma_start(out[0:P, cols], staged[0][:, cols])
-            nc.scalar.activation(staged[1][:, cols], windows[1][:, cols], IDENTITY, bias=bias[:, 1:2])
-            nc.scalar.dma_start(out[P : 2 * P, cols], staged[1][:, cols])
+        nc.scalar.activation(staged[0][:], windows[0][:], IDENTITY, bias=bias[:, 0:1])
+        nc.scalar.dma_start(out[0:P, :], staged[0][:])
+        nc.vector.tensor_scalar(staged[1][:], windows[1][:], bias[:, 1:2], None, ADD)
+        nc.sync.dma_start(out[P : 2 * P, :], staged[1][:])

@@ -13,6 +13,8 @@ N = 64
 K_BLOCKS = K // P
 M_BLOCKS = M // P
 
+WARMING_MATMULS = 2
+
 FLOPS = 2 * K * M * N
 
 
@@ -22,6 +24,12 @@ def tile_scatter_matmul_kernel(tc, base, x, w, b, offs, out):
         tc.tile_pool(name="held", bufs=1) as held,
         tc.psum_pool(name="psum", bufs=1) as psum,
     ):
+        zeros = held.tile([P, S], BF16, name="zeros")
+        nc.vector.memset(zeros[:], 0.0)
+        unread = psum.tile([P, S], F32, name="unread")
+        for i in range(WARMING_MATMULS):
+            nc.tensor.matmul(unread[:], zeros[:, 0:P], zeros[:], start=True, stop=True)
+
         ident = held.tile([P, P], BF16, name="ident")
         make_identity(nc, ident[:])
 

@@ -41,9 +41,9 @@ def tile_scatter_matmul_kernel(tc, base, x, w, b, offs, out):
         nc.sync.dma_start(offsets[:], offs)
 
         w_tile = held.tile([P, K_BLOCKS, M], BF16, name="w_tile")
-        nc.sync.dma_start(w_tile[:], w.rearrange("(kb p) m -> p kb m", p=P))
+        nc.sync.dma_start(w_tile[:], w.rearrange("(p kb) m -> p kb m", kb=K_BLOCKS))
         x_tile = held.tile([P, K_BLOCKS, N], BF16, name="x_tile")
-        nc.scalar.dma_start(x_tile[:], x.rearrange("(kb p) n -> p kb n", p=P))
+        nc.scalar.dma_start(x_tile[:], x.rearrange("(p kb) n -> p kb n", kb=K_BLOCKS))
 
         bias = held.tile([P, M_BLOCKS], F32, name="bias")
         with nc.allow_non_contiguous_dma(reason="one float32 to a partition and block"):

@@ -13,7 +13,7 @@ N = 64
 K_BLOCKS = K // P
 M_BLOCKS = M // P
 
-WARMING_MATMULS = 2
+WARMING_MATMULS = 3
 
 FLOPS = 2 * K * M * N
 
@@ -24,11 +24,17 @@ def tile_scatter_matmul_kernel(tc, base, x, w, b, offs, out):
         tc.tile_pool(name="held", bufs=1) as held,
         tc.psum_pool(name="psum", bufs=1) as psum,
     ):
-        zeros = held.tile([P, S], BF16, name="zeros")
+        zeros = held.tile([P, P], BF16, name="zeros")
         nc.vector.memset(zeros[:], 0.0)
-        unread = psum.tile([P, S], F32, name="unread")
+        unread = psum.tile([P, S // P, P], F32, name="unread")
         for i in range(WARMING_MATMULS):
-            nc.tensor.matmul(unread[:], zeros[:, 0:P], zeros[:], start=True, stop=True)
+            nc.tensor.matmul(
+                unread[:],
+                zeros[:],
+                zeros[:].unsqueeze(1).to_broadcast([P, S // P, P]),
+                start=True,
+                stop=True,
+            )
 
         ident = held.tile([P, P], BF16, name="ident")
         make_identity(nc, ident[:])

@@ -1,8 +1,7 @@
 import concourse.mybir as mybir
-from concourse.masks import make_identity
 
 BF16, F32, U16 = mybir.dt.bfloat16, mybir.dt.float32, mybir.dt.uint16
-ADD = mybir.AluOpType.add
+ADD, MULT, IS_EQUAL = mybir.AluOpType.add, mybir.AluOpType.mult, mybir.AluOpType.is_equal
 IDENTITY = mybir.ActivationFunctionType.Identity
 
 P = 128
@@ -12,6 +11,7 @@ M = 256
 N = 64
 K_BLOCKS = K // P
 M_BLOCKS = M // P
+SQUARE = 32
 
 WARMING_MATMULS = 3
 
@@ -36,8 +36,21 @@ def tile_scatter_matmul_kernel(tc, base, x, w, b, offs, out):
                 stop=True,
             )
 
+        ones = held.tile([P, SQUARE], F32, name="ones")
+        nc.vector.memset(ones[:], 1.0)
+        counted = held.tile([P, SQUARE], F32, name="counted", align_bytes=64)
+        nc.vector.tensor_tensor_scan(counted[:], ones[:], ones[:], 0.0, MULT, ADD)
+        turned = held.tile([P, SQUARE], F32, name="turned", align_bytes=64)
+        nc.vector.transpose(turned[:], counted[:])
         ident = held.tile([P, P], BF16, name="ident")
-        make_identity(nc, ident[:])
+        nc.vector.memset(ident[:], 0.0)
+        for q in range(0, P, SQUARE):
+            nc.vector.tensor_tensor(
+                ident[q : q + SQUARE, q : q + SQUARE],
+                counted[q : q + SQUARE, :],
+                turned[q : q + SQUARE, :],
+                IS_EQUAL,
+            )
 
         base_tiles = [held.tile([P, S], BF16, name=f"base{mb}") for mb in range(M_BLOCKS)]
         nc.sync.dma_start(base_tiles[0][:], base[0:P, :])

import concourse.mybir as mybir

BF16, F32, U16 = mybir.dt.bfloat16, mybir.dt.float32, mybir.dt.uint16
ADD, MULT, IS_EQUAL = mybir.AluOpType.add, mybir.AluOpType.mult, mybir.AluOpType.is_equal
IDENTITY = mybir.ActivationFunctionType.Identity

P = 128
S = 512
K = 256
M = 256
N = 64
K_BLOCKS = K // P
M_BLOCKS = M // P
SQUARE = 32

WARMING_MATMULS = 3

FLOPS = 2 * K * M * N


def tile_scatter_matmul_kernel(tc, base, x, w, b, offs, out):
    nc = tc.nc
    with (
        tc.tile_pool(name="held", bufs=1) as held,
        tc.psum_pool(name="psum", bufs=1) as psum,
    ):
        zeros = held.tile([P, P], BF16, name="zeros")
        nc.vector.memset(zeros[:], 0.0)
        unread = psum.tile([P, S // P, P], F32, name="unread")
        for i in range(WARMING_MATMULS):
            nc.tensor.matmul(
                unread[:],
                zeros[:],
                zeros[:].unsqueeze(1).to_broadcast([P, S // P, P]),
                start=True,
                stop=True,
            )

        ones = held.tile([P, SQUARE], F32, name="ones")
        nc.vector.memset(ones[:], 1.0)
        counted = held.tile([P, SQUARE], F32, name="counted", align_bytes=64)
        nc.vector.tensor_tensor_scan(counted[:], ones[:], ones[:], 0.0, MULT, ADD)
        turned = held.tile([P, SQUARE], F32, name="turned", align_bytes=64)
        nc.vector.transpose(turned[:], counted[:])
        ident = held.tile([P, P], BF16, name="ident")
        nc.vector.memset(ident[:], 0.0)
        for q in range(0, P, SQUARE):
            nc.vector.tensor_tensor(
                ident[q : q + SQUARE, q : q + SQUARE],
                counted[q : q + SQUARE, :],
                turned[q : q + SQUARE, :],
                IS_EQUAL,
            )

        base_tiles = [held.tile([P, S], BF16, name=f"base{mb}") for mb in range(M_BLOCKS)]
        nc.sync.dma_start(base_tiles[0][:], base[0:P, :])
        nc.scalar.dma_start(base_tiles[1][:], base[P : 2 * P, :])

        offsets = held.tile([P, N // 16], U16, name="offsets")
        nc.sync.dma_start(offsets[:], offs)

        w_tile = held.tile([P, K_BLOCKS, M], BF16, name="w_tile")
        nc.sync.dma_start(w_tile[:], w.rearrange("(p kb) m -> p kb m", kb=K_BLOCKS))
        x_tile = held.tile([P, K_BLOCKS, N], BF16, name="x_tile")
        nc.scalar.dma_start(x_tile[:], x.rearrange("(p kb) n -> p kb n", kb=K_BLOCKS))

        bias = held.tile([P, M_BLOCKS], F32, name="bias")
        with nc.allow_non_contiguous_dma(reason="one float32 to a partition and block"):
            nc.scalar.dma_start(bias[:], b.rearrange("(mb p) o -> p (mb o)", p=P))

        spare = held.tile([P, 2], F32, name="spare")
        nc.vector.memset(spare[:, 0:1], 0.0)
        nc.scalar.activation(spare[:, 1:2], spare[:, 0:1], IDENTITY)

        windows = [psum.tile([P, S], F32, name=f"window{mb}") for mb in range(M_BLOCKS)]
        for mb in range(M_BLOCKS):
            nc.tensor.matmul(windows[mb][:], ident[:], base_tiles[mb][:], start=True, stop=False)

        for mb in range(M_BLOCKS):
            for kb in range(K_BLOCKS):
                nc.tensor.matmul(
                    windows[mb][:].indirect(offsets[:]),
                    w_tile[:, kb, mb * P : (mb + 1) * P],
                    x_tile[:, kb, :],
                    start=False,
                    stop=(kb == K_BLOCKS - 1),
                )

        staged = [held.tile([P, S], F32, name=f"staged{mb}") for mb in range(M_BLOCKS)]
        nc.scalar.activation(staged[0][:], windows[0][:], IDENTITY, bias=bias[:, 0:1])
        nc.scalar.dma_start(out[0:P, :], staged[0][:])
        nc.vector.tensor_scalar(staged[1][:], windows[1][:], bias[:, 1:2], None, ADD)
        nc.sync.dma_start(out[P : 2 * P, :], staged[1][:])
